import numpy as np
import ml_dtypes


def mxq(x, axis, fmt="e4m3"):
    dtype, down = {"e4m3": (ml_dtypes.float8_e4m3fn, 7), "e5m2": (ml_dtypes.float8_e5m2, 14)}[fmt]
    v = np.moveaxis(np.asarray(x, np.float32).astype(ml_dtypes.bfloat16).astype(np.float64), axis, -1)
    blocks = v.reshape(v.shape[:-1] + (-1, 32))
    amax = np.abs(blocks).max(-1, keepdims=True)
    byte = np.maximum(np.where(amax > 0, np.frexp(amax)[1] - 1 + 127, 0) - down, 1)
    scale = np.exp2(byte - 127.0)
    codes = (blocks / scale).astype(np.float32).astype(dtype).astype(np.float64)
    return np.moveaxis((codes * scale).reshape(v.shape), -1, axis)


WIDE = False


def mx_kscale(k):
    if not WIDE:
        return np.ones(k)
    levels = np.array([10, -10, 5, -5, 0])
    if k % 512:
        return np.exp2(np.random.permutation(np.resize(levels, k // 32))).repeat(32)
    a = np.empty((k // 512, 16))
    for p in range(k // 512):
        a[p, :8] = np.random.permutation(np.resize(levels, 8))
        for g in range(8):
            far = levels[np.abs(levels - a[p, g]) >= 10]
            a[p, g + 8] = far[np.random.randint(len(far))]
    return np.exp2(a.ravel()).repeat(32)


def f64(x):
    return np.asarray(x).astype(np.float64)


def striped(idx):
    return np.tile(idx.reshape(-1, 16).T, (8, 1)).astype(np.uint16)


def unstriped(offs):
    return offs[:16].T.reshape(-1).astype(np.int64)


def striped8(idx):
    return np.concatenate([x.reshape(-1, 16).T for x in idx]).astype(np.uint16)


def runs(offs, k):
    lists = np.stack([offs[16 * r : 16 * r + 16].T.reshape(-1) for r in range(8)]).astype(np.int64)
    return lists[np.arange(k) % 512 // 64]


def pack_weight(w):
    k, n = w.shape
    w = f64(np.asarray(w, np.float32).astype(ml_dtypes.bfloat16)).reshape(k // 32, 32, n)
    amax = np.abs(w).max(1)
    byte = np.clip(np.where(amax > 0, np.frexp(amax)[1] - 1 + 127 - 7, 1), 1, 254)
    scaled = (w * np.exp2(127.0 - byte)[:, None, :]).reshape(k, n).astype(np.float32)
    words = np.ascontiguousarray(scaled.reshape(k // 512, 128, 4, n).transpose(0, 1, 3, 2)).astype(ml_dtypes.float8_e4m3fn).view(np.uint8)
    return words, np.ascontiguousarray(byte.astype(np.uint8).reshape(k // 512, 16, n))


def unpack_weight(words, scales):
    g, p, n, _ = words.shape
    vals = np.ascontiguousarray(words).view(ml_dtypes.float8_e4m3fn).astype(np.float64) * np.repeat(np.exp2(scales.astype(np.float64) - 127.0), 8, axis=1)[..., None]
    return vals.transpose(0, 1, 3, 2).reshape(g * 512, n)


def sigmoid(v):
    return 1.0 / (1.0 + np.exp(-np.maximum(v, -700.0)))


K, T, S, N, H = 512, 2048, 512, 512, 512


def setup_inputs():
    n = np.random.standard_normal
    s = mx_kscale(K)[:, None]
    u = mx_kscale(H)
    packed_xT = pack_weight(n((K, T)) * s)
    return {
        "x_words": packed_xT[0],
        "x_scales": packed_xT[1],
        "w1": (n((K, H)) / np.sqrt(K) / s).astype(np.float32),
        "w2": (n((K, H)) / np.sqrt(K) / s).astype(np.float32),
        "w3": (n((K, H)) / np.sqrt(K) / s).astype(np.float32),
        "tau": np.random.uniform(0.3, 0.9, (H, 1)).astype(np.float32),
        "gn": (np.random.uniform(0.5, 1.5, (H, 1)) * u[:, None]).astype(np.float32),
        "w4": (n((H, N)) / np.sqrt(H) / u[:, None]).astype(np.float32),
        "sl": np.random.uniform(1.0, 2.0, (N, 1)).astype(np.float32),
        "th": (0.5 * n((N, 1))).astype(np.float32),
        "offs": striped(np.random.permutation(T)[:S]),
        "two": striped(np.random.permutation(T)[:S]),
        "three": striped(np.random.permutation(T)[:S]),
        "n1": striped(np.random.permutation(S)),
        "n2": striped(np.random.permutation(S)),
        "n3": striped(np.random.permutation(S)),
        "n4": striped(np.random.permutation(S)),
        "n5": striped8(np.stack([np.random.permutation(S) for _ in range(8)])),
        "n6": striped8(np.stack([np.random.permutation(S) for _ in range(8)])),
        "n7": striped8(np.stack([np.random.permutation(S) for _ in range(8)])),
    }


def reference(x_words, x_scales, w1, w2, w3, tau, gn, w4, sl, th, offs, two, three, n1, n2, n3, n4, n5, n6, n7):
    x_three = unpack_weight(x_words, x_scales)[:, unstriped(three)]
    b = mxq(f64(w3), 0, "e4m3").T @ x_three
    top = b.max(axis=1, keepdims=True)
    ea = np.exp(f64(tau) * (b[:, unstriped(n3)] - top))
    xq = unpack_weight(x_words, x_scales)[:, unstriped(offs)]
    y = mxq(f64(w1), 0, "e4m3").T @ xq
    x_two = unpack_weight(x_words, x_scales)[:, unstriped(two)]
    d = mxq(f64(w2), 0, "e4m3").T @ x_two
    m1 = (y - y[:, unstriped(n1)]) / (np.abs(d) + np.abs(d[:, unstriped(n2)]) + 0.5)
    z = f64(gn) * ((2.0 * ea) * (m1 - m1[:, unstriped(n4)]) - (0.5 * b))
    h = mxq(f64(w4), 0, "e4m3").T @ mxq(z, 0, "e4m3")
    own = sigmoid(f64(sl) * (h - f64(th)))
    sg = sigmoid(f64(sl) * (h[np.arange(N)[:, None], runs(n5, N)] - f64(th)))
    return (h[np.arange(N)[:, None], runs(n6, N)]) * own + (h[np.arange(N)[:, None], runs(n7, N)]) * sg

@@ -1,0 +1,254 @@
+from contextlib import ExitStack
+
+import concourse.mybir as mybir
+
+K, T, S, H, N = 512, 2048, 512, 512, 512
+FLOPS = 2 * (3 * K * H * S + H * N * S)
+
+F32 = mybir.dt.float32
+BF16 = mybir.dt.bfloat16
+I32 = mybir.dt.int32
+U32 = mybir.dt.uint32
+U16 = mybir.dt.uint16
+U8 = mybir.dt.uint8
+FP8X4 = mybir.dt.float8_e4m3fn_x4
+ACT = mybir.ActivationFunctionType
+MULT = mybir.AluOpType.mult
+ADD = mybir.AluOpType.add
+SUB = mybir.AluOpType.subtract
+MAX = mybir.AluOpType.max
+
+P = 128
+PACK = 4
+HALF = S // 2
+HALVES = [slice(0, HALF), slice(HALF, S)]
+LIST_HALVES = [slice(0, HALF // 16), slice(HALF // 16, S // 16)]
+
+
+def tile_picked_trionormbpxbemx_none_p_kernel(
+    tc, x_words, x_scales, w1, w2, w3, tau, gn, w4, sl, th, offs, two, three, n1, n2, n3, n4, n5, n6, n7, out
+):
+    nc = tc.nc
+    with ExitStack() as ctx:
+        keep = ctx.enter_context(tc.tile_pool(name="keep", bufs=1))
+        psum = ctx.enter_context(tc.psum_pool(name="psum", bufs=1))
+
+        def load_list(name, src):
+            tile = keep.tile([P, S // 16], U16, name="list_" + name)
+            nc.sync.dma_start(tile[:], src)
+            return tile
+
+        def load_weight(name, src, pieces=1):
+            width = H // pieces
+            tiles = []
+            for i in range(pieces):
+                tile = keep.tile([P, PACK, width], F32, name="raw_%s_%d" % (name, i))
+                nc.sync.dma_start(tile[:], src.rearrange("(p j) c -> p j c", j=PACK)[:, :, i * width : (i + 1) * width])
+                tiles.append(tile)
+            return tiles
+
+        def load_column(name, src):
+            tile = keep.tile([P, PACK], F32, name="col_" + name)
+            nc.sync.dma_start(tile[:], src.rearrange("(p t) o -> p (t o)", t=PACK))
+            return tile
+
+        def planes(name, dtype=F32):
+            return [keep.tile([P, S], dtype, name="%s%d" % (name, t), align_bytes=64) for t in range(PACK)]
+
+        def bank(index):
+            return psum.tile([P, S], F32, name="bank%d" % index)
+
+        x_scale_table = keep.tile([P, T], U8, name="x_scale_table")
+        nc.vector.memset(x_scale_table[:].bitcast(I32), 0)
+        x_scale_rows = keep.tile([P, T], U8, name="x_scale_rows")
+        l_two = load_list("two", two)
+        for q in range(4):
+            nc.sync.dma_start(
+                x_scale_rows[32 * q : 32 * q + 4, :].bitcast(I32), x_scales[0, 4 * q : 4 * q + 4, :].bitcast(I32)
+            )
+        l_offs = load_list("offs", offs)
+        l_three = load_list("three", three)
+        raw2 = load_weight("w2", w2)
+        x_word_table = keep.tile([P, T], I32, name="x_word_table")
+        nc.sync.dma_start(x_word_table[:], x_words[0].rearrange("p c r -> p (c r)").bitcast(I32))
+        raw1 = load_weight("w1", w1, 2)
+        l_n2 = load_list("n2", n2)
+        l_n1 = load_list("n1", n1)
+        raw3 = load_weight("w3", w3)
+        tau_c = load_column("tau", tau)
+        gn_c = load_column("gn", gn)
+        l_n3 = load_list("n3", n3)
+        l_n4 = load_list("n4", n4)
+        raw4 = load_weight("w4", w4)
+        sl_c = load_column("sl", sl)
+        th_c = load_column("th", th)
+        l_n5 = load_list("n5", n5)
+        l_n6 = load_list("n6", n6)
+        l_n7 = load_list("n7", n7)
+
+        def pick_scales(name, lst):
+            tile = keep.tile([P, S], U8, name="xs_" + name, align_bytes=64)
+            nc.vector.tensor_copy(tile[:], x_scale_table[:].indirect(lst[:]))
+            return tile
+
+        def pick_words(name, lst, tag):
+            tile = keep.tile([P, S], U32, name="xw_" + name, tag=tag, align_bytes=64)
+            nc.vector.tensor_copy(tile[:], x_word_table[:].bitcast(U32).indirect(lst[:]))
+            return tile
+
+        def round_weight(name, raw, copies):
+            dealt = keep.tile([P, PACK * H], BF16, name="bf_" + name, tag="bf_" + name, align_bytes=64)
+            dst = dealt[:].rearrange("p (t m j) -> p m j t", t=PACK, j=PACK)
+            width = P // len(copies)
+            per_tile = len(copies) // len(raw)
+            for i, copy in enumerate(copies):
+                src = raw[i // per_tile][:].rearrange("p j (m t) -> p m j t", t=PACK)
+                first = i % per_tile * width
+                copy(dst[:, i * width : (i + 1) * width], src[:, first : first + width])
+            return dealt
+
+        def quantise_weight(name, dealt):
+            codes = keep.tile([P, H], U32, name="codes_" + name, align_bytes=64)
+            scales = keep.tile([P, H], U8, name="scales_" + name, align_bytes=64)
+            nc.vector.quantize_mx(out=codes[:].bitcast(FP8X4), scales=scales[:], in_=dealt[:])
+            return codes, scales
+
+        def product(acc, weight, t, words, scales):
+            cols = slice(t * P, (t + 1) * P)
+            nc.tensor.matmul_mx(
+                out=acc,
+                lhsT=weight[0][:, cols].bitcast(FP8X4),
+                lhsT_scale=weight[1][:, cols],
+                rhs=words.bitcast(FP8X4),
+                rhs_scale=scales,
+                start=True,
+                stop=True,
+            )
+
+        for q in range(4):
+            rows = slice(32 * q, 32 * q + 4)
+            nc.vector.tensor_copy(x_scale_table[rows, :].bitcast(I32), x_scale_rows[rows, :].bitcast(I32))
+        xs_two = pick_scales("two", l_two)
+        xs_offs = pick_scales("offs", l_offs)
+        xs_three = pick_scales("three", l_three)
+        bf2 = round_weight("w2", raw2, [nc.scalar.copy])
+        xw_two = pick_words("two", l_two, "xw_two")
+        q2 = quantise_weight("w2", bf2)
+
+        size = planes("size")
+        size_again = planes("size_again")
+        den = keep.tile([P, PACK, S], F32, name="den")
+        for t in range(PACK):
+            acc = bank(t)
+            product(acc[:], q2, t, xw_two[:], xs_two[:])
+            nc.scalar.activation(size[t][:], acc[:], ACT.Abs)
+        xw_offs = pick_words("offs", l_offs, "bf_w2")
+        bf1 = round_weight("w1", raw1, [nc.scalar.copy, nc.vector.tensor_copy])
+        q1 = quantise_weight("w1", bf1)
+
+        y = planes("y")
+        num = planes("num")
+        for t in range(PACK):
+            acc = bank(PACK + t)
+            product(acc[:], q1, t, xw_offs[:], xs_offs[:])
+            nc.scalar.copy(y[t][:], acc[:])
+        for t in range(PACK):
+            nc.vector.tensor_copy(size_again[t][:], size[t][:])
+            for cols, entries in zip(HALVES, LIST_HALVES):
+                nc.vector.tensor_tensor(
+                    den[:, t, cols], size[t][:].indirect(l_n2[:, entries]), size_again[t][:, cols], ADD
+                )
+        for t in range(PACK):
+            for cols, entries in zip(HALVES, LIST_HALVES):
+                nc.scalar.activation(num[t][:, cols], y[t][:].indirect(l_n1[:, entries]), ACT.Copy)
+            nc.vector.tensor_tensor(num[t][:], y[t][:], num[t][:], SUB)
+        nc.scalar.activation(den[:], den[:], ACT.Ln, bias=0.5)
+        for t in range(PACK):
+            nc.scalar.activation(den[:, t, :], den[:, t, :], ACT.Exp, scale=-1.0)
+
+        xw_three = pick_words("three", l_three, "bf_w1")
+        bf3 = round_weight("w3", raw3, [nc.vector.tensor_copy] * 2)
+        neg_tau = keep.tile([P, PACK], F32, name="neg_tau")
+        gain_ea = keep.tile([P, PACK], F32, name="gain_ea")
+        gain_b = keep.tile([P, PACK], F32, name="gain_b")
+        sig_bias = keep.tile([P, PACK], F32, name="sig_bias")
+        nc.vector.tensor_scalar(neg_tau[:], tau_c[:], -1.0, None, MULT)
+        nc.vector.tensor_scalar(gain_ea[:], gn_c[:], 2.0, None, MULT)
+        nc.vector.tensor_scalar(gain_b[:], gn_c[:], -0.5, None, MULT)
+        q3 = quantise_weight("w3", bf3)
+        b = planes("b")
+        top = keep.tile([P, PACK], F32, name="top")
+        exp_bias = keep.tile([P, PACK], F32, name="exp_bias")
+        for t in range(PACK):
+            acc = bank(t)
+            product(acc[:], q3, t, xw_three[:], xs_three[:])
+            nc.vector.tensor_scalar(b[t][:], acc[:], 1.0, None, MULT, MAX, accum_out=top[:, t : t + 1])
+            nc.vector.tensor_tensor(exp_bias[:, t : t + 1], top[:, t : t + 1], neg_tau[:, t : t + 1], MULT)
+        nc.vector.scalar_tensor_tensor(sig_bias[:], sl_c[:], -1.0, th_c[:], MULT, MULT)
+        bf4 = round_weight("w4", raw4, [nc.vector.tensor_copy] * 2)
+        q4 = quantise_weight("w4", bf4)
+
+        m1 = planes("m1")
+        ea = planes("ea")
+        work = planes("work")
+        z = keep.tile([P, PACK, S], BF16, name="z")
+        for t in range(PACK):
+            row = slice(t, t + 1)
+            nc.vector.tensor_tensor(m1[t][:], num[t][:], den[:, t, :], MULT)
+            for cols, entries in zip(HALVES, LIST_HALVES):
+                nc.scalar.activation(
+                    ea[t][:, cols], b[t][:].indirect(l_n3[:, entries]), ACT.Exp, bias=exp_bias[:, row], scale=tau_c[:, row]
+                )
+            for cols, entries in zip(HALVES, LIST_HALVES):
+                nc.scalar.activation(work[t][:, cols], m1[t][:].indirect(l_n4[:, entries]), ACT.Copy)
+            for cols in HALVES:
+                nc.vector.tensor_tensor(work[t][:, cols], m1[t][:, cols], work[t][:, cols], SUB)
+            for cols in HALVES:
+                nc.vector.scalar_tensor_tensor(
+                    work[t][:, cols], work[t][:, cols], gain_ea[:, row], ea[t][:, cols], MULT, MULT
+                )
+            for cols in HALVES:
+                nc.vector.scalar_tensor_tensor(z[:, t, cols], b[t][:, cols], gain_b[:, row], work[t][:, cols], MULT, ADD)
+
+        z_codes = []
+        z_scales = []
+        for i, cols in enumerate(HALVES):
+            woven = keep.tile([P, HALF, PACK], BF16, name="woven%d" % i, align_bytes=64)
+            [nc.scalar.copy, nc.vector.tensor_copy][i](
+                woven[:].rearrange("p (c i) t -> p c t i", i=4), z[:, :, cols].rearrange("p t (c i) -> p c t i", i=4)
+            )
+            z_codes.append(keep.tile([P, HALF], U32, name="z_codes%d" % i, align_bytes=64))
+            z_scales.append(keep.tile([P, HALF], U8, name="z_scales%d" % i, align_bytes=64))
+            nc.vector.quantize_mx(
+                out=z_codes[i][:].bitcast(FP8X4), scales=z_scales[i][:], in_=woven[:].rearrange("p c t -> p (c t)")
+            )
+
+        h = planes("h")
+        own = planes("own")
+        sg = planes("sg")
+        far = planes("far")
+        res = planes("res")
+        out_rows = out.rearrange("(p t) j -> p t j", t=PACK)
+        accs = [bank(PACK + t) for t in range(PACK)]
+        for i, cols in enumerate(HALVES):
+            for t in range(PACK):
+                product(accs[t][:, cols], q4, t, z_codes[i][:], z_scales[i][:])
+        for t in range(PACK):
+            row = slice(t, t + 1)
+            if t == 0:
+                nc.scalar.activation(own[1][:], accs[1][:], ACT.Sigmoid, bias=sig_bias[:, 1:2], scale=sl_c[:, 1:2])
+            nc.vector.tensor_copy(h[t][:], accs[t][:])
+            if t != 1:
+                nc.scalar.activation(own[t][:], h[t][:], ACT.Sigmoid, bias=sig_bias[:, row], scale=sl_c[:, row])
+            for cols, entries in zip(HALVES, LIST_HALVES):
+                nc.scalar.activation(far[t][:, cols], h[t][:].indirect(l_n7[:, entries]), ACT.Copy)
+                nc.scalar.activation(
+                    sg[t][:, cols], h[t][:].indirect(l_n5[:, entries]), ACT.Sigmoid, bias=sig_bias[:, row], scale=sl_c[:, row]
+                )
+            for cols, entries in zip(HALVES, LIST_HALVES):
+                nc.vector.tensor_tensor(res[t][:, cols], h[t][:].indirect(l_n6[:, entries]), own[t][:, cols], MULT)
+            for cols in HALVES:
+                nc.vector.tensor_tensor(far[t][:, cols], far[t][:, cols], sg[t][:, cols], MULT)
+            for cols in HALVES:
+                nc.vector.tensor_tensor(res[t][:, cols], res[t][:, cols], far[t][:, cols], ADD)
+                nc.sync.dma_start(out_rows[:, t, cols], res[t][:, cols])

@@ -38,11 +38,12 @@ def tile_picked_trionormbpxbemx_none_p_kernel(
             nc.sync.dma_start(tile[:], src)
             return tile
 
-        def load_weight(name, src, pieces=1):
+        def load_weight(name, src, pieces=1, tag=None):
             width = H // pieces
             tiles = []
             for i in range(pieces):
-                tile = keep.tile([P, PACK, width], F32, name="raw_%s_%d" % (name, i))
+                label = "raw_%s_%d" % (name, i)
+                tile = keep.tile([P, PACK, width], F32, name=label, tag=tag or label, align_bytes=64)
                 nc.sync.dma_start(tile[:], src.rearrange("(p j) c -> p j c", j=PACK)[:, :, i * width : (i + 1) * width])
                 tiles.append(tile)
             return tiles
@@ -52,12 +53,18 @@ def tile_picked_trionormbpxbemx_none_p_kernel(
             nc.sync.dma_start(tile[:], src.rearrange("(p t) o -> p (t o)", t=PACK))
             return tile
 
-        def planes(name, dtype=F32):
-            return [keep.tile([P, S], dtype, name="%s%d" % (name, t), align_bytes=64) for t in range(PACK)]
+        def plane(name, tag=None):
+            return keep.tile([P, S], F32, name=name, tag=tag or name, align_bytes=64)
+
+        def planes(name):
+            return [plane("%s%d" % (name, t)) for t in range(PACK)]
 
         def bank(index):
             return psum.tile([P, S], F32, name="bank%d" % index)
 
+        warm = keep.tile([P, 1], F32, name="warm")
+        nc.gpsimd.memset(warm[:], 1.0)
+        nc.scalar.activation(warm[:], warm[:], ACT.Ln, bias=0.5)
         x_scale_table = keep.tile([P, T], U8, name="x_scale_table")
         nc.vector.memset(x_scale_table[:].bitcast(I32), 0)
         x_scale_rows = keep.tile([P, T], U8, name="x_scale_rows")
@@ -66,12 +73,12 @@ def tile_picked_trionormbpxbemx_none_p_kernel(
             nc.sync.dma_start(
                 x_scale_rows[32 * q : 32 * q + 4, :].bitcast(I32), x_scales[0, 4 * q : 4 * q + 4, :].bitcast(I32)
             )
-        l_offs = load_list("offs", offs)
-        l_three = load_list("three", three)
-        raw2 = load_weight("w2", w2)
         x_word_table = keep.tile([P, T], I32, name="x_word_table")
         nc.sync.dma_start(x_word_table[:], x_words[0].rearrange("p c r -> p (c r)").bitcast(I32))
+        l_offs = load_list("offs", offs)
+        raw2 = load_weight("w2", w2, 2)
         raw1 = load_weight("w1", w1, 2)
+        l_three = load_list("three", three)
         l_n2 = load_list("n2", n2)
         l_n1 = load_list("n1", n1)
         raw3 = load_weight("w3", w3)
@@ -86,8 +93,8 @@ def tile_picked_trionormbpxbemx_none_p_kernel(
         l_n6 = load_list("n6", n6)
         l_n7 = load_list("n7", n7)
 
-        def pick_scales(name, lst):
-            tile = keep.tile([P, S], U8, name="xs_" + name, align_bytes=64)
+        def pick_scales(name, lst, tag):
+            tile = keep.tile([P, S], U8, name="xs_" + name, tag=tag, align_bytes=64)
             nc.vector.tensor_copy(tile[:], x_scale_table[:].indirect(lst[:]))
             return tile
 
@@ -96,8 +103,11 @@ def tile_picked_trionormbpxbemx_none_p_kernel(
             nc.vector.tensor_copy(tile[:], x_word_table[:].bitcast(U32).indirect(lst[:]))
             return tile
 
-        def round_weight(name, raw, copies):
-            dealt = keep.tile([P, PACK * H], BF16, name="bf_" + name, tag="bf_" + name, align_bytes=64)
+        def gpsimd_round(dst, src):
+            nc.gpsimd.tensor_scalar(dst, src, 1.0, 0.0, MULT, ADD)
+
+        def round_weight(name, raw, copies, tag=None):
+            dealt = keep.tile([P, PACK * H], BF16, name="bf_" + name, tag=tag or "bf_" + name, align_bytes=64)
             dst = dealt[:].rearrange("p (t m j) -> p m j t", t=PACK, j=PACK)
             width = P // len(copies)
             per_tile = len(copies) // len(raw)
@@ -128,15 +138,19 @@ def tile_picked_trionormbpxbemx_none_p_kernel(
         for q in range(4):
             rows = slice(32 * q, 32 * q + 4)
             nc.vector.tensor_copy(x_scale_table[rows, :].bitcast(I32), x_scale_rows[rows, :].bitcast(I32))
-        xs_two = pick_scales("two", l_two)
-        xs_offs = pick_scales("offs", l_offs)
-        xs_three = pick_scales("three", l_three)
-        bf2 = round_weight("w2", raw2, [nc.scalar.copy])
+        xs_two = pick_scales("two", l_two, "xs_two")
         xw_two = pick_words("two", l_two, "xw_two")
+        xs_offs = pick_scales("offs", l_offs, "xs_offs")
+        bf2 = round_weight("w2", raw2, [nc.scalar.copy, nc.vector.tensor_copy])
         q2 = quantise_weight("w2", bf2)
 
+        def wide(name, count=PACK):
+            return [keep.tile([P, 2 * S], F32, name="%s%d" % (name, t), align_bytes=64) for t in range(count)]
+
+        left, right = slice(0, S), slice(S, 2 * S)
+
         size = planes("size")
-        size_again = planes("size_again")
+        y = wide("y")
         den = keep.tile([P, PACK, S], F32, name="den")
         for t in range(PACK):
             acc = bank(t)
@@ -146,75 +160,80 @@ def tile_picked_trionormbpxbemx_none_p_kernel(
         bf1 = round_weight("w1", raw1, [nc.scalar.copy, nc.vector.tensor_copy])
         q1 = quantise_weight("w1", bf1)
 
-        y = planes("y")
+        b = wide("b")
         num = planes("num")
+        y_acc = [bank(PACK + t) for t in range(PACK)]
         for t in range(PACK):
-            acc = bank(PACK + t)
-            product(acc[:], q1, t, xw_offs[:], xs_offs[:])
-            nc.scalar.copy(y[t][:], acc[:])
+            product(y_acc[t][:], q1, t, xw_offs[:], xs_offs[:])
+            nc.scalar.copy(y[t][:, left], y_acc[t][:])
         for t in range(PACK):
-            nc.vector.tensor_copy(size_again[t][:], size[t][:])
+            nc.vector.tensor_copy(y[t][:, right], size[t][:])
             for cols, entries in zip(HALVES, LIST_HALVES):
                 nc.vector.tensor_tensor(
-                    den[:, t, cols], size[t][:].indirect(l_n2[:, entries]), size_again[t][:, cols], ADD
+                    den[:, t, cols], size[t][:].indirect(l_n2[:, entries]), y[t][:, right][:, cols], ADD
                 )
+        xs_three = pick_scales("three", l_three, "bf_w1")
+        xw_three = pick_words("three", l_three, "size0")
         for t in range(PACK):
-            for cols, entries in zip(HALVES, LIST_HALVES):
-                nc.scalar.activation(num[t][:, cols], y[t][:].indirect(l_n1[:, entries]), ACT.Copy)
-            nc.vector.tensor_tensor(num[t][:], y[t][:], num[t][:], SUB)
+            nc.scalar.activation(b[t][:, right], y[t][:].indirect(l_n1[:]), ACT.Copy)
+            nc.vector.tensor_tensor(num[t][:], y[t][:, left], b[t][:, right], SUB)
+        m1 = wide("m1")
         nc.scalar.activation(den[:], den[:], ACT.Ln, bias=0.5)
         for t in range(PACK):
-            nc.scalar.activation(den[:, t, :], den[:, t, :], ACT.Exp, scale=-1.0)
+            nc.scalar.activation(m1[t][:, right], den[:, t, :], ACT.Exp, scale=-1.0)
 
-        xw_three = pick_words("three", l_three, "bf_w1")
-        bf3 = round_weight("w3", raw3, [nc.vector.tensor_copy] * 2)
         neg_tau = keep.tile([P, PACK], F32, name="neg_tau")
         gain_ea = keep.tile([P, PACK], F32, name="gain_ea")
         gain_b = keep.tile([P, PACK], F32, name="gain_b")
         sig_bias = keep.tile([P, PACK], F32, name="sig_bias")
-        nc.vector.tensor_scalar(neg_tau[:], tau_c[:], -1.0, None, MULT)
-        nc.vector.tensor_scalar(gain_ea[:], gn_c[:], 2.0, None, MULT)
-        nc.vector.tensor_scalar(gain_b[:], gn_c[:], -0.5, None, MULT)
+        neg_sl = keep.tile([P, PACK], F32, name="neg_sl")
+        nc.gpsimd.tensor_scalar(neg_tau[:], tau_c[:], -1.0, 0.0, MULT, ADD)
+        nc.gpsimd.tensor_scalar(gain_ea[:], gn_c[:], 2.0, 0.0, MULT, ADD)
+        nc.gpsimd.tensor_scalar(gain_b[:], gn_c[:], -0.5, 0.0, MULT, ADD)
+        nc.gpsimd.tensor_scalar(neg_sl[:], sl_c[:], -1.0, 0.0, MULT, ADD)
+        nc.gpsimd.tensor_tensor(sig_bias[:], neg_sl[:], th_c[:], MULT)
+        bf3 = round_weight("w3", raw3, [nc.vector.tensor_copy] * 2)
         q3 = quantise_weight("w3", bf3)
-        b = planes("b")
         top = keep.tile([P, PACK], F32, name="top")
         exp_bias = keep.tile([P, PACK], F32, name="exp_bias")
         for t in range(PACK):
             acc = bank(t)
             product(acc[:], q3, t, xw_three[:], xs_three[:])
-            nc.vector.tensor_scalar(b[t][:], acc[:], 1.0, None, MULT, MAX, accum_out=top[:, t : t + 1])
-            nc.vector.tensor_tensor(exp_bias[:, t : t + 1], top[:, t : t + 1], neg_tau[:, t : t + 1], MULT)
-        nc.vector.scalar_tensor_tensor(sig_bias[:], sl_c[:], -1.0, th_c[:], MULT, MULT)
-        bf4 = round_weight("w4", raw4, [nc.vector.tensor_copy] * 2)
-        q4 = quantise_weight("w4", bf4)
+            nc.vector.tensor_scalar(b[t][:, left], acc[:], 1.0, None, MULT, MAX, accum_out=top[:, t : t + 1])
+            nc.gpsimd.tensor_tensor(exp_bias[:, t : t + 1], top[:, t : t + 1], neg_tau[:, t : t + 1], MULT)
 
-        m1 = planes("m1")
-        ea = planes("ea")
-        work = planes("work")
+        h = wide("h", PACK - 1)
         z = keep.tile([P, PACK, S], BF16, name="z")
         for t in range(PACK):
+            nc.vector.tensor_tensor(m1[t][:, left], num[t][:], m1[t][:, right], MULT)
+        for t in range(PACK):
             row = slice(t, t + 1)
-            nc.vector.tensor_tensor(m1[t][:], num[t][:], den[:, t, :], MULT)
-            for cols, entries in zip(HALVES, LIST_HALVES):
+            ea = plane("ea%d" % t, "num%d" % (t - 1) if t else None)
+            work = h[t][:, right] if t < PACK - 1 else plane("work_last")
+            pieces = [slice(0, S)] if t < PACK - 1 else HALVES
+            for piece in pieces:
+                entries = slice(piece.start // 16, piece.stop // 16)
+                nc.scalar.activation(work[:, piece], m1[t][:].indirect(l_n4[:, entries]), ACT.Copy)
                 nc.scalar.activation(
-                    ea[t][:, cols], b[t][:].indirect(l_n3[:, entries]), ACT.Exp, bias=exp_bias[:, row], scale=tau_c[:, row]
+                    ea[:, piece], b[t][:].indirect(l_n3[:, entries]), ACT.Exp, bias=exp_bias[:, row], scale=tau_c[:, row]
                 )
-            for cols, entries in zip(HALVES, LIST_HALVES):
-                nc.scalar.activation(work[t][:, cols], m1[t][:].indirect(l_n4[:, entries]), ACT.Copy)
-            for cols in HALVES:
-                nc.vector.tensor_tensor(work[t][:, cols], m1[t][:, cols], work[t][:, cols], SUB)
-            for cols in HALVES:
-                nc.vector.scalar_tensor_tensor(
-                    work[t][:, cols], work[t][:, cols], gain_ea[:, row], ea[t][:, cols], MULT, MULT
-                )
-            for cols in HALVES:
-                nc.vector.scalar_tensor_tensor(z[:, t, cols], b[t][:, cols], gain_b[:, row], work[t][:, cols], MULT, ADD)
+                halves = [cols for cols in HALVES if piece.start <= cols.start < piece.stop]
+                for cols in halves:
+                    nc.vector.tensor_tensor(work[:, cols], m1[t][:, cols], work[:, cols], SUB)
+                for cols in halves:
+                    nc.vector.scalar_tensor_tensor(work[:, cols], work[:, cols], gain_ea[:, row], ea[:, cols], MULT, MULT)
+                for cols in halves:
+                    nc.vector.scalar_tensor_tensor(z[:, t, cols], b[t][:, cols], gain_b[:, row], work[:, cols], MULT, ADD)
+            if t == 0:
+                bf4 = round_weight("w4", raw4, [nc.vector.tensor_copy] * 4)
+            if t == 1:
+                q4 = quantise_weight("w4", bf4)
 
         z_codes = []
         z_scales = []
         for i, cols in enumerate(HALVES):
             woven = keep.tile([P, HALF, PACK], BF16, name="woven%d" % i, align_bytes=64)
-            [nc.scalar.copy, nc.vector.tensor_copy][i](
+            nc.vector.tensor_copy(
                 woven[:].rearrange("p (c i) t -> p c t i", i=4), z[:, :, cols].rearrange("p t (c i) -> p c t i", i=4)
             )
             z_codes.append(keep.tile([P, HALF], U32, name="z_codes%d" % i, align_bytes=64))
@@ -223,32 +242,37 @@ def tile_picked_trionormbpxbemx_none_p_kernel(
                 out=z_codes[i][:].bitcast(FP8X4), scales=z_scales[i][:], in_=woven[:].rearrange("p c t -> p (c t)")
             )
 
-        h = planes("h")
         own = planes("own")
         sg = planes("sg")
         far = planes("far")
         res = planes("res")
+        h_last = plane("h_last")
         out_rows = out.rearrange("(p t) j -> p t j", t=PACK)
         accs = [bank(PACK + t) for t in range(PACK)]
         for i, cols in enumerate(HALVES):
-            for t in range(PACK):
+            for t in (1, 0, 2, 3):
                 product(accs[t][:, cols], q4, t, z_codes[i][:], z_scales[i][:])
         for t in range(PACK):
             row = slice(t, t + 1)
+            last = t == PACK - 1
+            window = h_last if last else h[t]
             if t == 0:
                 nc.scalar.activation(own[1][:], accs[1][:], ACT.Sigmoid, bias=sig_bias[:, 1:2], scale=sl_c[:, 1:2])
-            nc.vector.tensor_copy(h[t][:], accs[t][:])
+            nc.vector.tensor_copy(window[:, left], accs[t][:])
             if t != 1:
-                nc.scalar.activation(own[t][:], h[t][:], ACT.Sigmoid, bias=sig_bias[:, row], scale=sl_c[:, row])
-            for cols, entries in zip(HALVES, LIST_HALVES):
-                nc.scalar.activation(far[t][:, cols], h[t][:].indirect(l_n7[:, entries]), ACT.Copy)
+                nc.scalar.activation(own[t][:], window[:, left], ACT.Sigmoid, bias=sig_bias[:, row], scale=sl_c[:, row])
+            pieces = [HALVES[0], slice(HALF, 3 * S // 4), slice(3 * S // 4, S)] if last else [slice(0, S)]
+            for piece in pieces:
+                entries = slice(piece.start // 16, piece.stop // 16)
+                nc.scalar.activation(far[t][:, piece], window[:].indirect(l_n7[:, entries]), ACT.Copy)
                 nc.scalar.activation(
-                    sg[t][:, cols], h[t][:].indirect(l_n5[:, entries]), ACT.Sigmoid, bias=sig_bias[:, row], scale=sl_c[:, row]
+                    sg[t][:, piece], window[:].indirect(l_n5[:, entries]), ACT.Sigmoid, bias=sig_bias[:, row], scale=sl_c[:, row]
                 )
-            for cols, entries in zip(HALVES, LIST_HALVES):
-                nc.vector.tensor_tensor(res[t][:, cols], h[t][:].indirect(l_n6[:, entries]), own[t][:, cols], MULT)
-            for cols in HALVES:
+            for piece in HALVES if last else pieces:
+                entries = slice(piece.start // 16, piece.stop // 16)
+                nc.vector.tensor_tensor(res[t][:, piece], window[:].indirect(l_n6[:, entries]), own[t][:, piece], MULT)
+            for cols in pieces if last else HALVES:
                 nc.vector.tensor_tensor(far[t][:, cols], far[t][:, cols], sg[t][:, cols], MULT)
-            for cols in HALVES:
+            for cols in pieces if last else HALVES:
                 nc.vector.tensor_tensor(res[t][:, cols], res[t][:, cols], far[t][:, cols], ADD)
                 nc.sync.dma_start(out_rows[:, t, cols], res[t][:, cols])

from contextlib import ExitStack

import concourse.mybir as mybir

K, T, S, H, N = 512, 2048, 512, 512, 512
FLOPS = 2 * (3 * K * H * S + H * N * S)

F32 = mybir.dt.float32
BF16 = mybir.dt.bfloat16
I32 = mybir.dt.int32
U32 = mybir.dt.uint32
U16 = mybir.dt.uint16
U8 = mybir.dt.uint8
FP8X4 = mybir.dt.float8_e4m3fn_x4
ACT = mybir.ActivationFunctionType
MULT = mybir.AluOpType.mult
ADD = mybir.AluOpType.add
SUB = mybir.AluOpType.subtract
MAX = mybir.AluOpType.max

P = 128
PACK = 4
HALF = S // 2
HALVES = [slice(0, HALF), slice(HALF, S)]
LIST_HALVES = [slice(0, HALF // 16), slice(HALF // 16, S // 16)]


def tile_picked_trionormbpxbemx_none_p_kernel(
    tc, x_words, x_scales, w1, w2, w3, tau, gn, w4, sl, th, offs, two, three, n1, n2, n3, n4, n5, n6, n7, out
):
    nc = tc.nc
    with ExitStack() as ctx:
        keep = ctx.enter_context(tc.tile_pool(name="keep", bufs=1))
        psum = ctx.enter_context(tc.psum_pool(name="psum", bufs=1))

        def load_list(name, src):
            tile = keep.tile([P, S // 16], U16, name="list_" + name)
            nc.sync.dma_start(tile[:], src)
            return tile

        def load_weight(name, src, pieces=1, tag=None):
            width = H // pieces
            tiles = []
            for i in range(pieces):
                label = "raw_%s_%d" % (name, i)
                tile = keep.tile([P, PACK, width], F32, name=label, tag=tag or label, align_bytes=64)
                nc.sync.dma_start(tile[:], src.rearrange("(p j) c -> p j c", j=PACK)[:, :, i * width : (i + 1) * width])
                tiles.append(tile)
            return tiles

        def load_column(name, src):
            tile = keep.tile([P, PACK], F32, name="col_" + name)
            nc.sync.dma_start(tile[:], src.rearrange("(p t) o -> p (t o)", t=PACK))
            return tile

        def plane(name, tag=None):
            return keep.tile([P, S], F32, name=name, tag=tag or name, align_bytes=64)

        def planes(name):
            return [plane("%s%d" % (name, t)) for t in range(PACK)]

        def bank(index):
            return psum.tile([P, S], F32, name="bank%d" % index)

        warm = keep.tile([P, 1], F32, name="warm")
        nc.gpsimd.memset(warm[:], 1.0)
        nc.scalar.activation(warm[:], warm[:], ACT.Ln, bias=0.5)
        x_scale_table = keep.tile([P, T], U8, name="x_scale_table")
        nc.vector.memset(x_scale_table[:].bitcast(I32), 0)
        x_scale_rows = keep.tile([P, T], U8, name="x_scale_rows")
        l_two = load_list("two", two)
        for q in range(4):
            nc.sync.dma_start(
                x_scale_rows[32 * q : 32 * q + 4, :].bitcast(I32), x_scales[0, 4 * q : 4 * q + 4, :].bitcast(I32)
            )
        x_word_table = keep.tile([P, T], I32, name="x_word_table")
        nc.sync.dma_start(x_word_table[:], x_words[0].rearrange("p c r -> p (c r)").bitcast(I32))
        l_offs = load_list("offs", offs)
        raw2 = load_weight("w2", w2, 2)
        raw1 = load_weight("w1", w1, 2)
        l_three = load_list("three", three)
        l_n2 = load_list("n2", n2)
        l_n1 = load_list("n1", n1)
        raw3 = load_weight("w3", w3)
        tau_c = load_column("tau", tau)
        gn_c = load_column("gn", gn)
        l_n3 = load_list("n3", n3)
        l_n4 = load_list("n4", n4)
        raw4 = load_weight("w4", w4)
        sl_c = load_column("sl", sl)
        th_c = load_column("th", th)
        l_n5 = load_list("n5", n5)
        l_n6 = load_list("n6", n6)
        l_n7 = load_list("n7", n7)

        def pick_scales(name, lst, tag):
            tile = keep.tile([P, S], U8, name="xs_" + name, tag=tag, align_bytes=64)
            nc.vector.tensor_copy(tile[:], x_scale_table[:].indirect(lst[:]))
            return tile

        def pick_words(name, lst, tag):
            tile = keep.tile([P, S], U32, name="xw_" + name, tag=tag, align_bytes=64)
            nc.vector.tensor_copy(tile[:], x_word_table[:].bitcast(U32).indirect(lst[:]))
            return tile

        def gpsimd_round(dst, src):
            nc.gpsimd.tensor_scalar(dst, src, 1.0, 0.0, MULT, ADD)

        def round_weight(name, raw, copies, tag=None):
            dealt = keep.tile([P, PACK * H], BF16, name="bf_" + name, tag=tag or "bf_" + name, align_bytes=64)
            dst = dealt[:].rearrange("p (t m j) -> p m j t", t=PACK, j=PACK)
            width = P // len(copies)
            per_tile = len(copies) // len(raw)
            for i, copy in enumerate(copies):
                src = raw[i // per_tile][:].rearrange("p j (m t) -> p m j t", t=PACK)
                first = i % per_tile * width
                copy(dst[:, i * width : (i + 1) * width], src[:, first : first + width])
            return dealt

        def quantise_weight(name, dealt):
            codes = keep.tile([P, H], U32, name="codes_" + name, align_bytes=64)
            scales = keep.tile([P, H], U8, name="scales_" + name, align_bytes=64)
            nc.vector.quantize_mx(out=codes[:].bitcast(FP8X4), scales=scales[:], in_=dealt[:])
            return codes, scales

        def product(acc, weight, t, words, scales):
            cols = slice(t * P, (t + 1) * P)
            nc.tensor.matmul_mx(
                out=acc,
                lhsT=weight[0][:, cols].bitcast(FP8X4),
                lhsT_scale=weight[1][:, cols],
                rhs=words.bitcast(FP8X4),
                rhs_scale=scales,
                start=True,
                stop=True,
            )

        for q in range(4):
            rows = slice(32 * q, 32 * q + 4)
            nc.vector.tensor_copy(x_scale_table[rows, :].bitcast(I32), x_scale_rows[rows, :].bitcast(I32))
        xs_two = pick_scales("two", l_two, "xs_two")
        xw_two = pick_words("two", l_two, "xw_two")
        xs_offs = pick_scales("offs", l_offs, "xs_offs")
        bf2 = round_weight("w2", raw2, [nc.scalar.copy, nc.vector.tensor_copy])
        q2 = quantise_weight("w2", bf2)

        def wide(name, count=PACK):
            return [keep.tile([P, 2 * S], F32, name="%s%d" % (name, t), align_bytes=64) for t in range(count)]

        left, right = slice(0, S), slice(S, 2 * S)

        size = planes("size")
        y = wide("y")
        den = keep.tile([P, PACK, S], F32, name="den")
        for t in range(PACK):
            acc = bank(t)
            product(acc[:], q2, t, xw_two[:], xs_two[:])
            nc.scalar.activation(size[t][:], acc[:], ACT.Abs)
        xw_offs = pick_words("offs", l_offs, "bf_w2")
        bf1 = round_weight("w1", raw1, [nc.scalar.copy, nc.vector.tensor_copy])
        q1 = quantise_weight("w1", bf1)

        b = wide("b")
        num = planes("num")
        y_acc = [bank(PACK + t) for t in range(PACK)]
        for t in range(PACK):
            product(y_acc[t][:], q1, t, xw_offs[:], xs_offs[:])
            nc.scalar.copy(y[t][:, left], y_acc[t][:])
        for t in range(PACK):
            nc.vector.tensor_copy(y[t][:, right], size[t][:])
            for cols, entries in zip(HALVES, LIST_HALVES):
                nc.vector.tensor_tensor(
                    den[:, t, cols], size[t][:].indirect(l_n2[:, entries]), y[t][:, right][:, cols], ADD
                )
        xs_three = pick_scales("three", l_three, "bf_w1")
        xw_three = pick_words("three", l_three, "size0")
        for t in range(PACK):
            nc.scalar.activation(b[t][:, right], y[t][:].indirect(l_n1[:]), ACT.Copy)
            nc.vector.tensor_tensor(num[t][:], y[t][:, left], b[t][:, right], SUB)
        m1 = wide("m1")
        nc.scalar.activation(den[:], den[:], ACT.Ln, bias=0.5)
        for t in range(PACK):
            nc.scalar.activation(m1[t][:, right], den[:, t, :], ACT.Exp, scale=-1.0)

        neg_tau = keep.tile([P, PACK], F32, name="neg_tau")
        gain_ea = keep.tile([P, PACK], F32, name="gain_ea")
        gain_b = keep.tile([P, PACK], F32, name="gain_b")
        sig_bias = keep.tile([P, PACK], F32, name="sig_bias")
        neg_sl = keep.tile([P, PACK], F32, name="neg_sl")
        nc.gpsimd.tensor_scalar(neg_tau[:], tau_c[:], -1.0, 0.0, MULT, ADD)
        nc.gpsimd.tensor_scalar(gain_ea[:], gn_c[:], 2.0, 0.0, MULT, ADD)
        nc.gpsimd.tensor_scalar(gain_b[:], gn_c[:], -0.5, 0.0, MULT, ADD)
        nc.gpsimd.tensor_scalar(neg_sl[:], sl_c[:], -1.0, 0.0, MULT, ADD)
        nc.gpsimd.tensor_tensor(sig_bias[:], neg_sl[:], th_c[:], MULT)
        bf3 = round_weight("w3", raw3, [nc.vector.tensor_copy] * 2)
        q3 = quantise_weight("w3", bf3)
        top = keep.tile([P, PACK], F32, name="top")
        exp_bias = keep.tile([P, PACK], F32, name="exp_bias")
        for t in range(PACK):
            acc = bank(t)
            product(acc[:], q3, t, xw_three[:], xs_three[:])
            nc.vector.tensor_scalar(b[t][:, left], acc[:], 1.0, None, MULT, MAX, accum_out=top[:, t : t + 1])
            nc.gpsimd.tensor_tensor(exp_bias[:, t : t + 1], top[:, t : t + 1], neg_tau[:, t : t + 1], MULT)

        h = wide("h", PACK - 1)
        z = keep.tile([P, PACK, S], BF16, name="z")
        for t in range(PACK):
            nc.vector.tensor_tensor(m1[t][:, left], num[t][:], m1[t][:, right], MULT)
        for t in range(PACK):
            row = slice(t, t + 1)
            ea = plane("ea%d" % t, "num%d" % (t - 1) if t else None)
            work = h[t][:, right] if t < PACK - 1 else plane("work_last")
            pieces = [slice(0, S)] if t < PACK - 1 else HALVES
            for piece in pieces:
                entries = slice(piece.start // 16, piece.stop // 16)
                nc.scalar.activation(work[:, piece], m1[t][:].indirect(l_n4[:, entries]), ACT.Copy)
                nc.scalar.activation(
                    ea[:, piece], b[t][:].indirect(l_n3[:, entries]), ACT.Exp, bias=exp_bias[:, row], scale=tau_c[:, row]
                )
                halves = [cols for cols in HALVES if piece.start <= cols.start < piece.stop]
                for cols in halves:
                    nc.vector.tensor_tensor(work[:, cols], m1[t][:, cols], work[:, cols], SUB)
                for cols in halves:
                    nc.vector.scalar_tensor_tensor(work[:, cols], work[:, cols], gain_ea[:, row], ea[:, cols], MULT, MULT)
                for cols in halves:
                    nc.vector.scalar_tensor_tensor(z[:, t, cols], b[t][:, cols], gain_b[:, row], work[:, cols], MULT, ADD)
            if t == 0:
                bf4 = round_weight("w4", raw4, [nc.vector.tensor_copy] * 4)
            if t == 1:
                q4 = quantise_weight("w4", bf4)

        z_codes = []
        z_scales = []
        for i, cols in enumerate(HALVES):
            woven = keep.tile([P, HALF, PACK], BF16, name="woven%d" % i, align_bytes=64)
            nc.vector.tensor_copy(
                woven[:].rearrange("p (c i) t -> p c t i", i=4), z[:, :, cols].rearrange("p t (c i) -> p c t i", i=4)
            )
            z_codes.append(keep.tile([P, HALF], U32, name="z_codes%d" % i, align_bytes=64))
            z_scales.append(keep.tile([P, HALF], U8, name="z_scales%d" % i, align_bytes=64))
            nc.vector.quantize_mx(
                out=z_codes[i][:].bitcast(FP8X4), scales=z_scales[i][:], in_=woven[:].rearrange("p c t -> p (c t)")
            )

        own = planes("own")
        sg = planes("sg")
        far = planes("far")
        res = planes("res")
        h_last = plane("h_last")
        out_rows = out.rearrange("(p t) j -> p t j", t=PACK)
        accs = [bank(PACK + t) for t in range(PACK)]
        for i, cols in enumerate(HALVES):
            for t in (1, 0, 2, 3):
                product(accs[t][:, cols], q4, t, z_codes[i][:], z_scales[i][:])
        for t in range(PACK):
            row = slice(t, t + 1)
            last = t == PACK - 1
            window = h_last if last else h[t]
            if t == 0:
                nc.scalar.activation(own[1][:], accs[1][:], ACT.Sigmoid, bias=sig_bias[:, 1:2], scale=sl_c[:, 1:2])
            nc.vector.tensor_copy(window[:, left], accs[t][:])
            if t != 1:
                nc.scalar.activation(own[t][:], window[:, left], ACT.Sigmoid, bias=sig_bias[:, row], scale=sl_c[:, row])
            pieces = [HALVES[0], slice(HALF, 3 * S // 4), slice(3 * S // 4, S)] if last else [slice(0, S)]
            for piece in pieces:
                entries = slice(piece.start // 16, piece.stop // 16)
                nc.scalar.activation(far[t][:, piece], window[:].indirect(l_n7[:, entries]), ACT.Copy)
                nc.scalar.activation(
                    sg[t][:, piece], window[:].indirect(l_n5[:, entries]), ACT.Sigmoid, bias=sig_bias[:, row], scale=sl_c[:, row]
                )
            for piece in HALVES if last else pieces:
                entries = slice(piece.start // 16, piece.stop // 16)
                nc.vector.tensor_tensor(res[t][:, piece], window[:].indirect(l_n6[:, entries]), own[t][:, piece], MULT)
            for cols in pieces if last else HALVES:
                nc.vector.tensor_tensor(far[t][:, cols], far[t][:, cols], sg[t][:, cols], MULT)
            for cols in pieces if last else HALVES:
                nc.vector.tensor_tensor(res[t][:, cols], res[t][:, cols], far[t][:, cols], ADD)
                nc.sync.dma_start(out_rows[:, t, cols], res[t][:, cols])
